import numpy as np
import ml_dtypes


def mxq(x, axis, fmt="e4m3"):
    dtype, down = {"e4m3": (ml_dtypes.float8_e4m3fn, 7), "e5m2": (ml_dtypes.float8_e5m2, 14)}[fmt]
    v = np.moveaxis(np.asarray(x, np.float32).astype(ml_dtypes.bfloat16).astype(np.float64), axis, -1)
    blocks = v.reshape(v.shape[:-1] + (-1, 32))
    amax = np.abs(blocks).max(-1, keepdims=True)
    byte = np.maximum(np.where(amax > 0, np.frexp(amax)[1] - 1 + 127, 0) - down, 1)
    scale = np.exp2(byte - 127.0)
    codes = (blocks / scale).astype(np.float32).astype(dtype).astype(np.float64)
    return np.moveaxis((codes * scale).reshape(v.shape), -1, axis)


WIDE = False


def mx_kscale(k):
    if not WIDE:
        return np.ones(k)
    levels = np.array([24, -24, 12, -12, 0])
    if k % 512:
        return np.exp2(np.random.permutation(np.resize(levels, k // 32))).repeat(32)
    a = np.empty((k // 512, 16))
    for p in range(k // 512):
        a[p, :8] = np.random.permutation(np.resize(levels, 8))
        for g in range(8):
            far = levels[np.abs(levels - a[p, g]) >= 10]
            a[p, g + 8] = far[np.random.randint(len(far))]
    return np.exp2(a.ravel()).repeat(32)


def f64(x):
    return np.asarray(x).astype(np.float64)


def striped8(idx):
    return np.concatenate([v.reshape(-1, 16).T for v in idx]).astype(np.uint16)


def unstriped8(offs):
    return np.stack([offs[16 * g:16 * g + 16].T.reshape(-1) for g in range(8)]).astype(np.int64)


E2M1 = np.array([0.0, 0.5, 1.0, 1.5, 2.0, 3.0, 4.0, 6.0, -0.0, -0.5, -1.0, -1.5, -2.0, -3.0, -4.0, -6.0])


def pack_weight(w, fmt):
    k, n = w.shape
    w = f64(np.asarray(w, np.float32).astype(ml_dtypes.bfloat16)).reshape(k // 32, 32, n)
    amax = np.abs(w).max(1)
    if fmt == "e4m3":
        byte = np.frexp(amax)[1] - 1 + 127 - 7
    else:
        mant, ex = np.frexp(amax / 6.0)
        byte = np.where(mant > 0.5, ex, ex - 1) + 127
    byte = np.clip(np.where(amax > 0, byte, 1), 1, 254)
    scaled = (w * np.exp2(127.0 - byte)[:, None, :]).reshape(k, n).astype(np.float32)
    by_word = np.ascontiguousarray(scaled.reshape(k // 512, 128, 4, n).transpose(0, 1, 3, 2))
    if fmt == "e4m3":
        words = by_word.astype(ml_dtypes.float8_e4m3fn).view(np.uint8)
    else:
        c = by_word.astype(ml_dtypes.float4_e2m1fn).view(np.uint8) & 0xF
        words = (c[..., 0::2] | (c[..., 1::2] << 4)).reshape(k // 512, 128, 2 * n)
    return np.ascontiguousarray(words), np.ascontiguousarray(byte.astype(np.uint8).reshape(k // 512, 16, n))


def unpack_weight(words, scales, fmt):
    g, _, n = scales.shape
    words = np.ascontiguousarray(words).reshape(g, 128, n, -1)
    if fmt == "e4m3":
        vals = words.view(ml_dtypes.float8_e4m3fn).astype(np.float64)
    else:
        nib = np.empty((g, 128, n, 4), np.uint8)
        nib[..., 0::2] = words & 0xF
        nib[..., 1::2] = words >> 4
        vals = E2M1[nib]
    vals = vals * np.repeat(np.exp2(scales.astype(np.float64) - 127.0), 8, axis=1)[..., None]
    return vals.transpose(0, 1, 3, 2).reshape(g * 512, n)


def planes(y):
    n, m = y.shape
    v = y.astype(np.float32).astype(ml_dtypes.bfloat16).astype(np.float64).reshape(n // 32, 32, m)
    top = np.abs(v).max(1)
    byte = np.clip(np.where(top > 0, np.frexp(top)[1] - 1 + 127 - 7, 1), 1, 254)
    codes = (v * np.exp2(127.0 - byte)[:, None, :]).reshape(n, m).astype(np.float32).astype(ml_dtypes.float8_e4m3fn).view(np.uint8)
    words = codes.reshape(n // 512, 128, 4, m).transpose(0, 1, 3, 2)
    return np.ascontiguousarray(words), np.ascontiguousarray(byte.astype(np.uint8).reshape(n // 512, 16, m))


K, N, T, J = 512, 512, 2048, 512


def setup_inputs():
    n = np.random.standard_normal
    s = mx_kscale(K)[:, None]
    p_w = pack_weight(n((K, N)) / np.sqrt(K) / s, "e4m3")
    return {
        "xT": (n((K, T)) * s).astype(np.float32),
        "wgt": np.repeat(np.random.uniform(0.5, 2.0, (8, 2 * J)), 16, axis=0).astype(np.float32),
        "w_words": p_w[0],
        "w_scales": p_w[1],
        "res": (n((N, J))).astype(np.float32),
        "offs": striped8(np.stack([np.concatenate([np.random.permutation(T)[:J] for _ in range(2)]) for _ in range(8)])),
    }


def reference(xT, wgt, w_words, w_scales, res, offs):
    idx = unstriped8(offs)
    rows = np.arange(K)
    xg = f64(wgt)[rows // 4 % 128] * f64(xT)[rows[:, None], idx[rows % 512 // 64]]
    xT_ = mxq(xg, 0, "e4m3").reshape(K, 2, J)
    w_ = unpack_weight(w_words, w_scales, "e4m3")
    a0 = w_.T @ xT_[:, 0]
    a1 = w_.T @ xT_[:, 1]
    out_0 = f64(res) + np.abs(a0 - a1)
    return (out_0,) + planes(out_0)

@@ -1,0 +1,120 @@
+from contextlib import ExitStack
+
+import concourse.mybir as mybir
+
+K, N, T, J = 512, 512, 2048, 512
+PICKS = 2
+FLOPS = 2 * K * N * J * PICKS
+
+F32 = mybir.dt.float32
+BF16 = mybir.dt.bfloat16
+I32 = mybir.dt.int32
+U32 = mybir.dt.uint32
+U16 = mybir.dt.uint16
+U8 = mybir.dt.uint8
+FP8X4 = mybir.dt.float8_e4m3fn_x4
+ALU = mybir.AluOpType
+ACT = mybir.ActivationFunctionType
+
+P = 128
+PACK = 4
+GROUP = 16
+HALF = 256
+CH = 128
+LINE = 4
+
+
+def tile_list_span_resP_kernel(tc, xT, wgt, w_words, w_scales, res, offs, out_0, out_1, out_2):
+    nc = tc.nc
+    halves = J // HALF
+    chunks = J // CH
+    with ExitStack() as ctx:
+        keep = ctx.enter_context(tc.tile_pool(name="keep", bufs=1))
+        psum = ctx.enter_context(tc.psum_pool(name="psum", bufs=1))
+
+        offsets = keep.tile([P, PICKS * J // GROUP], U16, name="offsets")
+        nc.sync.dma_start(offsets[:], offs)
+
+        scales_raw = keep.tile([P, N], U8, name="scales_raw", align_bytes=64)
+        nc.vector.memset(scales_raw[:].bitcast(I32), 0)
+        for q in range(4):
+            nc.scalar.dma_start(out=scales_raw[32 * q : 32 * q + 4, :].bitcast(I32), in_=w_scales[0, 4 * q : 4 * q + 4, :].bitcast(I32))
+
+        x_rows = xT.rearrange("(p i) t -> p i t", i=PACK)
+        x_plane = [keep.tile([P, T], F32, name=f"x_plane{i}") for i in range(PACK)]
+        weight = [keep.tile([P, J], F32, name=f"weight{c}") for c in range(PICKS)]
+        nc.sync.dma_start(out=weight[0][:], in_=wgt[:, 0:J])
+        nc.sync.dma_start(out=x_plane[0][:], in_=x_rows[:, 0, :])
+        nc.sync.dma_start(out=weight[1][:], in_=wgt[:, J : 2 * J])
+        for i in range(1, PACK):
+            nc.sync.dma_start(out=x_plane[i][:], in_=x_rows[:, i, :])
+        words_raw = keep.tile([P, N], I32, name="words_raw", align_bytes=64)
+        nc.sync.dma_start(out=words_raw[:], in_=w_words[0].rearrange("p n t -> p (n t)").bitcast(I32))
+        res_rows = res.rearrange("(p i) j -> p i j", i=PACK)
+        res_half = [keep.tile([P, PACK, HALF], F32, name=f"res_half{h}") for h in range(halves)]
+        for h in range(halves):
+            nc.sync.dma_start(out=res_half[h][:], in_=res_rows[:, :, h * HALF : (h + 1) * HALF])
+
+        weight_neg = keep.tile([P, J], F32, name="weight_neg")
+        nc.scalar.activation(out=weight_neg[:], in_=weight[1][:], func=ACT.Copy, scale=-1.0)
+        signed = [weight[0], weight_neg]
+
+        w_scale = keep.tile([P, PACK, P], U8, name="w_scale", align_bytes=64)
+        nc.vector.tensor_copy(out=w_scale[:].rearrange("p t m -> p m t"), in_=scales_raw[:].rearrange("p (m t) -> p m t", t=PACK))
+
+        picked = [keep.tile([P, PACK, PICKS, HALF], F32, name=f"picked{h}") for h in range(halves)]
+
+        def gather(i, h):
+            for c in range(PICKS):
+                first = c * J + h * HALF
+                cols = offsets[:, first // GROUP : (first + HALF) // GROUP]
+                nc.vector.tensor_tensor(picked[h][:, i, c, :], x_plane[i][:].indirect(cols), signed[c][:, h * HALF : (h + 1) * HALF], ALU.mult)
+
+        for i in range(PACK):
+            for h in range(halves):
+                gather(i, h)
+
+        w_code = keep.tile([P, PACK, P], I32, name="w_code", align_bytes=64)
+        nc.vector.tensor_copy(out=w_code[:].rearrange("p t m -> p m t"), in_=words_raw[:].rearrange("p (m t) -> p m t", t=PACK))
+
+        out_rows = out_0.rearrange("(p i) j -> p i j", i=PACK)
+        out_words = out_1[0].rearrange("p j t -> p (j t)").bitcast(I32)
+        y_scale = keep.tile([P, J], U8, name="y_scale", align_bytes=64)
+        for s in range(chunks):
+            h, j0 = divmod(s * CH, HALF)
+            xb = keep.tile([P, PICKS * CH * PACK], BF16, name=f"xb{s}", align_bytes=64)
+            nc.scalar.copy(
+                out=xb[:].rearrange("p (c q e t) -> p c q t e", c=PICKS, e=LINE, t=PACK),
+                in_=picked[h][:, :, :, j0 : j0 + CH].rearrange("p t c (q e) -> p c q t e", e=LINE),
+            )
+            x_code = keep.tile([P, PICKS * CH], U32, name=f"x_code{s}", align_bytes=64)
+            x_scale = keep.tile([P, PICKS * CH], U8, name=f"x_scale{s}", align_bytes=64)
+            nc.vector.quantize_mx(out=x_code[:].bitcast(FP8X4), scales=x_scale[:], in_=xb[:])
+            acc = psum.tile([P, PACK, CH], F32, name=f"acc{s}")
+            for t in range(PACK):
+                for c in range(PICKS):
+                    nc.tensor.matmul_mx(
+                        out=acc[:, t, :],
+                        lhsT=w_code[:, t, :].bitcast(FP8X4),
+                        lhsT_scale=w_scale[:, t, :],
+                        rhs=x_code[:, c * CH : (c + 1) * CH].bitcast(FP8X4),
+                        rhs_scale=x_scale[:, c * CH : (c + 1) * CH],
+                        start=(c == 0),
+                        stop=(c == PICKS - 1),
+                    )
+            span = keep.tile([P, PACK, CH], F32, name=f"span{s}")
+            nc.scalar.activation(out=span[:], in_=acc[:], func=ACT.Abs)
+            y = keep.tile([P, PACK, CH], F32, name=f"y{s}")
+            nc.vector.tensor_tensor(y[:], span[:], res_half[h][:, :, j0 : j0 + CH], ALU.add)
+            nc.sync.dma_start(out=out_rows[:, :, s * CH : (s + 1) * CH], in_=y[:])
+            yb = keep.tile([P, CH * PACK], BF16, name=f"yb{s}", align_bytes=64)
+            nc.vector.tensor_copy(
+                out=yb[:].rearrange("p (q e t) -> p q t e", e=LINE, t=PACK),
+                in_=y[:].rearrange("p t (q e) -> p q t e", e=LINE),
+            )
+            y_code = keep.tile([P, CH], U32, name=f"y_code{s}", align_bytes=64)
+            nc.vector.quantize_mx(out=y_code[:].bitcast(FP8X4), scales=y_scale[:, s * CH : (s + 1) * CH], in_=yb[:])
+            nc.sync.dma_start(out=out_words[:, s * CH : (s + 1) * CH], in_=y_code[:].bitcast(I32))
+        for q in range(4):
+            eng = nc.sync if q == 0 else nc.scalar
+            eng.dma_start(out=out_2[0, 4 * q : 4 * q + 4, :].bitcast(I32), in_=y_scale[32 * q : 32 * q + 4, :].bitcast(I32))

@@ -19,9 +19,11 @@ ACT = mybir.ActivationFunctionType
 P = 128
 PACK = 4
 GROUP = 16
+HEADS = P // GROUP
 HALF = 256
 CH = 128
 LINE = 4
+LEAD = 2
 
 
 def tile_list_span_resP_kernel(tc, xT, wgt, w_words, w_scales, res, offs, out_0, out_1, out_2):
@@ -62,17 +64,43 @@ def tile_list_span_resP_kernel(tc, xT, wgt, w_words, w_scales, res, offs, out_0,
         w_scale = keep.tile([P, PACK, P], U8, name="w_scale", align_bytes=64)
         nc.vector.tensor_copy(out=w_scale[:].rearrange("p t m -> p m t"), in_=scales_raw[:].rearrange("p (m t) -> p m t", t=PACK))
 
-        picked = [keep.tile([P, PACK, PICKS, HALF], F32, name=f"picked{h}") for h in range(halves)]
+        early = [keep.tile([P, 2, J], F32, name=f"early{c}") for c in range(PICKS)]
+        plane_words = PICKS * CH
+        xb_words = PICKS * CH * PACK // 2
+        late, xb = [], []
+        shared = [keep.tile([P, plane_words + xb_words], F32, name=f"shared{s}", align_bytes=64) for s in range(chunks - LEAD)]
+        for s in range(chunks):
+            if s < LEAD:
+                own = keep.tile([P, 2 * plane_words], F32, name=f"late{s}")
+            else:
+                own = shared[s - LEAD]
+            late.append(own[:, 0 : 2 * plane_words].rearrange("p (t c j) -> p t c j", t=2, c=PICKS))
+            if s < chunks - LEAD:
+                staged = shared[s][:, plane_words:].bitcast(BF16)
+            else:
+                staged = keep.tile([P, 2 * xb_words], BF16, name=f"xb{s}", align_bytes=64)[:]
+            xb.append(staged.rearrange("p (c j t) -> p c j t", c=PICKS, t=PACK))
 
-        def gather(i, h):
+        def gather(dst, i, c, j0, width):
+            first = c * J + j0
+            cols = offsets[:, first // GROUP : (first + width) // GROUP]
+            nc.vector.tensor_tensor(dst, x_plane[i][:].indirect(cols), signed[c][:, j0 : j0 + width], ALU.mult)
+
+        for i in range(2):
             for c in range(PICKS):
-                first = c * J + h * HALF
-                cols = offsets[:, first // GROUP : (first + HALF) // GROUP]
-                nc.vector.tensor_tensor(picked[h][:, i, c, :], x_plane[i][:].indirect(cols), signed[c][:, h * HALF : (h + 1) * HALF], ALU.mult)
-
-        for i in range(PACK):
-            for h in range(halves):
-                gather(i, h)
+                gather(early[c][:, i, :], i, c, 0, J)
+        for c in range(PICKS):
+            for s in range(chunks):
+                nc.scalar.copy(
+                    out=xb[s][:, c, :, 0:2].rearrange("p (q e) t -> p q t e", e=LINE),
+                    in_=early[c][:, :, s * CH : (s + 1) * CH].rearrange("p t (q e) -> p q t e", e=LINE),
+                )
+        for s in range(chunks):
+            for c in range(PICKS):
+                gather(late[s][:, 0, c, :], 2, c, s * CH, CH)
+        for s in range(LEAD):
+            for c in range(PICKS):
+                gather(late[s][:, 1, c, :], 3, c, s * CH, CH)
 
         w_code = keep.tile([P, PACK, P], I32, name="w_code", align_bytes=64)
         nc.vector.tensor_copy(out=w_code[:].rearrange("p t m -> p m t"), in_=words_raw[:].rearrange("p (m t) -> p m t", t=PACK))
@@ -80,41 +108,76 @@ def tile_list_span_resP_kernel(tc, xT, wgt, w_words, w_scales, res, offs, out_0,
         out_rows = out_0.rearrange("(p i) j -> p i j", i=PACK)
         out_words = out_1[0].rearrange("p j t -> p (j t)").bitcast(I32)
         y_scale = keep.tile([P, J], U8, name="y_scale", align_bytes=64)
-        for s in range(chunks):
-            h, j0 = divmod(s * CH, HALF)
-            xb = keep.tile([P, PICKS * CH * PACK], BF16, name=f"xb{s}", align_bytes=64)
+        x_code = [keep.tile([P, PICKS * CH], U32, name=f"x_code{s}", align_bytes=64) for s in range(chunks)]
+        x_scale = [keep.tile([P, PICKS * CH], U8, name=f"x_scale{s}", align_bytes=64) for s in range(chunks)]
+        span = [keep.tile([P, PACK, CH], F32, name=f"span{s}") for s in range(chunks)]
+        y = [keep.tile([P, PACK, HALF], F32, name=f"y{h}") for h in range(halves)]
+        y_code = [keep.tile([P, HALF], U32, name=f"y_code{h}", align_bytes=64) for h in range(halves)]
+
+        def front(s):
             nc.scalar.copy(
-                out=xb[:].rearrange("p (c q e t) -> p c q t e", c=PICKS, e=LINE, t=PACK),
-                in_=picked[h][:, :, :, j0 : j0 + CH].rearrange("p t c (q e) -> p c q t e", e=LINE),
+                out=xb[s][:, :, :, 2:4].rearrange("p c (q e) t -> p c q t e", e=LINE),
+                in_=late[s].rearrange("p t c (q e) -> p c q t e", e=LINE),
             )
-            x_code = keep.tile([P, PICKS * CH], U32, name=f"x_code{s}", align_bytes=64)
-            x_scale = keep.tile([P, PICKS * CH], U8, name=f"x_scale{s}", align_bytes=64)
-            nc.vector.quantize_mx(out=x_code[:].bitcast(FP8X4), scales=x_scale[:], in_=xb[:])
-            acc = psum.tile([P, PACK, CH], F32, name=f"acc{s}")
-            for t in range(PACK):
+            nc.vector.quantize_mx(out=x_code[s][:].bitcast(FP8X4), scales=x_scale[s][:], in_=xb[s].rearrange("p c j t -> p (c j t)"))
+
+        def project(s, u):
+            acc = psum.tile([P, 2, CH], F32, name=f"acc{s}_{u}", tag=f"bank{2 * s + u}")
+            for t in range(2):
                 for c in range(PICKS):
                     nc.tensor.matmul_mx(
                         out=acc[:, t, :],
-                        lhsT=w_code[:, t, :].bitcast(FP8X4),
-                        lhsT_scale=w_scale[:, t, :],
-                        rhs=x_code[:, c * CH : (c + 1) * CH].bitcast(FP8X4),
-                        rhs_scale=x_scale[:, c * CH : (c + 1) * CH],
+                        lhsT=w_code[:, 2 * u + t, :].bitcast(FP8X4),
+                        lhsT_scale=w_scale[:, 2 * u + t, :],
+                        rhs=x_code[s][:, c * CH : (c + 1) * CH].bitcast(FP8X4),
+                        rhs_scale=x_scale[s][:, c * CH : (c + 1) * CH],
                         start=(c == 0),
                         stop=(c == PICKS - 1),
                     )
-            span = keep.tile([P, PACK, CH], F32, name=f"span{s}")
-            nc.scalar.activation(out=span[:], in_=acc[:], func=ACT.Abs)
-            y = keep.tile([P, PACK, CH], F32, name=f"y{s}")
-            nc.vector.tensor_tensor(y[:], span[:], res_half[h][:, :, j0 : j0 + CH], ALU.add)
-            nc.sync.dma_start(out=out_rows[:, :, s * CH : (s + 1) * CH], in_=y[:])
-            yb = keep.tile([P, CH * PACK], BF16, name=f"yb{s}", align_bytes=64)
-            nc.vector.tensor_copy(
+            nc.scalar.activation(out=span[s][:, 2 * u : 2 * u + 2, :], in_=acc[:], func=ACT.Abs)
+
+        def add(s, ts):
+            h, j0 = divmod(s * CH, HALF)
+            nc.vector.tensor_tensor(y[h][:, ts, j0 : j0 + CH], span[s][:, ts, :], res_half[h][:, ts, j0 : j0 + CH], ALU.add)
+
+        def pack(j, width, copy):
+            h, j0 = divmod(j, HALF)
+            yb = keep.tile([P, width * PACK], BF16, name=f"yb{j}", align_bytes=64)
+            copy(
                 out=yb[:].rearrange("p (q e t) -> p q t e", e=LINE, t=PACK),
-                in_=y[:].rearrange("p t (q e) -> p q t e", e=LINE),
+                in_=y[h][:, :, j0 : j0 + width].rearrange("p t (q e) -> p q t e", e=LINE),
             )
-            y_code = keep.tile([P, CH], U32, name=f"y_code{s}", align_bytes=64)
-            nc.vector.quantize_mx(out=y_code[:].bitcast(FP8X4), scales=y_scale[:, s * CH : (s + 1) * CH], in_=yb[:])
-            nc.sync.dma_start(out=out_words[:, s * CH : (s + 1) * CH], in_=y_code[:].bitcast(I32))
+            nc.vector.quantize_mx(out=y_code[h][:, j0 : j0 + width].bitcast(FP8X4), scales=y_scale[:, j : j + width], in_=yb[:])
+
+        def store_y(h):
+            nc.sync.dma_start(out=out_rows[:, :, h * HALF : (h + 1) * HALF], in_=y[h][:])
+
+        def store_words(h):
+            nc.sync.dma_start(out=out_words[:, h * HALF : (h + 1) * HALF], in_=y_code[h][:].bitcast(I32))
+
+        for s in range(chunks):
+            front(s)
+            if s + LEAD < chunks:
+                for c in range(PICKS):
+                    gather(late[s + LEAD][:, 1, c, :], 3, c, (s + LEAD) * CH, CH)
+        for s in range(chunks):
+            for u in range(2):
+                project(s, u)
+        whole = slice(0, PACK)
+        add(0, whole)
+        add(1, whole)
+        store_y(0)
+        add(2, whole)
+        add(3, slice(0, 2))
+        add(3, slice(2, 4))
+        store_y(1)
+        pack(0, CH, nc.scalar.copy)
+        pack(CH, CH, nc.scalar.copy)
+        store_words(0)
+        pack(2 * CH, CH, nc.scalar.copy)
+        pack(3 * CH, CH, nc.vector.tensor_copy)
+        store_words(1)
+
         for q in range(4):
             eng = nc.sync if q == 0 else nc.scalar
             eng.dma_start(out=out_2[0, 4 * q : 4 * q + 4, :].bitcast(I32), in_=y_scale[32 * q : 32 * q + 4, :].bitcast(I32))

@@ -23,7 +23,6 @@ HEADS = P // GROUP
 HALF = 256
 CH = 128
 LINE = 4
-LEAD = 2
 
 
 def tile_list_span_resP_kernel(tc, xT, wgt, w_words, w_scales, res, offs, out_0, out_1, out_2):
@@ -43,7 +42,7 @@ def tile_list_span_resP_kernel(tc, xT, wgt, w_words, w_scales, res, offs, out_0,
             nc.scalar.dma_start(out=scales_raw[32 * q : 32 * q + 4, :].bitcast(I32), in_=w_scales[0, 4 * q : 4 * q + 4, :].bitcast(I32))
 
         x_rows = xT.rearrange("(p i) t -> p i t", i=PACK)
-        x_plane = [keep.tile([P, T], F32, name=f"x_plane{i}") for i in range(PACK)]
+        x_plane = [keep.tile([P, T], F32, name=f"x_plane{i}", tag=f"x_plane{i}", align_bytes=64) for i in range(PACK)]
         weight = [keep.tile([P, J], F32, name=f"weight{c}") for c in range(PICKS)]
         nc.sync.dma_start(out=weight[0][:], in_=wgt[:, 0:J])
         nc.sync.dma_start(out=x_plane[0][:], in_=x_rows[:, 0, :])
@@ -61,25 +60,10 @@ def tile_list_span_resP_kernel(tc, xT, wgt, w_words, w_scales, res, offs, out_0,
         nc.scalar.activation(out=weight_neg[:], in_=weight[1][:], func=ACT.Copy, scale=-1.0)
         signed = [weight[0], weight_neg]
 
-        w_scale = keep.tile([P, PACK, P], U8, name="w_scale", align_bytes=64)
-        nc.vector.tensor_copy(out=w_scale[:].rearrange("p t m -> p m t"), in_=scales_raw[:].rearrange("p (m t) -> p m t", t=PACK))
 
         early = [keep.tile([P, 2, J], F32, name=f"early{c}") for c in range(PICKS)]
-        plane_words = PICKS * CH
-        xb_words = PICKS * CH * PACK // 2
-        late, xb = [], []
-        shared = [keep.tile([P, plane_words + xb_words], F32, name=f"shared{s}", align_bytes=64) for s in range(chunks - LEAD)]
-        for s in range(chunks):
-            if s < LEAD:
-                own = keep.tile([P, 2 * plane_words], F32, name=f"late{s}")
-            else:
-                own = shared[s - LEAD]
-            late.append(own[:, 0 : 2 * plane_words].rearrange("p (t c j) -> p t c j", t=2, c=PICKS))
-            if s < chunks - LEAD:
-                staged = shared[s][:, plane_words:].bitcast(BF16)
-            else:
-                staged = keep.tile([P, 2 * xb_words], BF16, name=f"xb{s}", align_bytes=64)[:]
-            xb.append(staged.rearrange("p (c j t) -> p c j t", c=PICKS, t=PACK))
+        late = keep.tile([P, 2, PICKS, J], F32, name="late")
+        xb = [keep.tile([P, PICKS, CH, PACK], BF16, name=f"xb{s}", align_bytes=64) for s in range(chunks)]
 
         def gather(dst, i, c, j0, width):
             first = c * J + j0
@@ -89,21 +73,28 @@ def tile_list_span_resP_kernel(tc, xT, wgt, w_words, w_scales, res, offs, out_0,
         for i in range(2):
             for c in range(PICKS):
                 gather(early[c][:, i, :], i, c, 0, J)
+        w_scale = keep.tile([P, PACK, P], U8, name="w_scale", tag="x_plane0", align_bytes=64)
+        nc.vector.tensor_copy(
+            out=w_scale[:].rearrange("p t (q e) -> p q t e", e=16),
+            in_=scales_raw[:].rearrange("p (q e t) -> p q t e", e=16, t=PACK),
+        )
         for c in range(PICKS):
             for s in range(chunks):
                 nc.scalar.copy(
                     out=xb[s][:, c, :, 0:2].rearrange("p (q e) t -> p q t e", e=LINE),
                     in_=early[c][:, :, s * CH : (s + 1) * CH].rearrange("p t (q e) -> p q t e", e=LINE),
                 )
-        for s in range(chunks):
+        for c in range(PICKS):
+            gather(late[:, 0, c, :], 2, c, 0, J)
+        for j0, width in ((0, CH), (CH, CH), (HALF, HALF)):
             for c in range(PICKS):
-                gather(late[s][:, 0, c, :], 2, c, s * CH, CH)
-        for s in range(LEAD):
-            for c in range(PICKS):
-                gather(late[s][:, 1, c, :], 3, c, s * CH, CH)
+                gather(late[:, 1, c, j0 : j0 + width], 3, c, j0, width)
 
         w_code = keep.tile([P, PACK, P], I32, name="w_code", align_bytes=64)
-        nc.vector.tensor_copy(out=w_code[:].rearrange("p t m -> p m t"), in_=words_raw[:].rearrange("p (m t) -> p m t", t=PACK))
+        nc.vector.tensor_copy(
+            out=w_code[:].rearrange("p t (q e) -> p q t e", e=LINE),
+            in_=words_raw[:].rearrange("p (q e t) -> p q t e", e=LINE, t=PACK),
+        )
 
         out_rows = out_0.rearrange("(p i) j -> p i j", i=PACK)
         out_words = out_1[0].rearrange("p j t -> p (j t)").bitcast(I32)
@@ -117,9 +108,9 @@ def tile_list_span_resP_kernel(tc, xT, wgt, w_words, w_scales, res, offs, out_0,
         def front(s):
             nc.scalar.copy(
                 out=xb[s][:, :, :, 2:4].rearrange("p c (q e) t -> p c q t e", e=LINE),
-                in_=late[s].rearrange("p t c (q e) -> p c q t e", e=LINE),
+                in_=late[:, :, :, s * CH : (s + 1) * CH].rearrange("p t c (q e) -> p c q t e", e=LINE),
             )
-            nc.vector.quantize_mx(out=x_code[s][:].bitcast(FP8X4), scales=x_scale[s][:], in_=xb[s].rearrange("p c j t -> p (c j t)"))
+            nc.vector.quantize_mx(out=x_code[s][:].bitcast(FP8X4), scales=x_scale[s][:], in_=xb[s][:].rearrange("p c j t -> p (c j t)"))
 
         def project(s, u):
             acc = psum.tile([P, 2, CH], F32, name=f"acc{s}_{u}", tag=f"bank{2 * s + u}")
@@ -157,9 +148,6 @@ def tile_list_span_resP_kernel(tc, xT, wgt, w_words, w_scales, res, offs, out_0,
 
         for s in range(chunks):
             front(s)
-            if s + LEAD < chunks:
-                for c in range(PICKS):
-                    gather(late[s + LEAD][:, 1, c, :], 3, c, (s + LEAD) * CH, CH)
         for s in range(chunks):
             for u in range(2):
                 project(s, u)
@@ -171,7 +159,7 @@ def tile_list_span_resP_kernel(tc, xT, wgt, w_words, w_scales, res, offs, out_0,
         add(3, slice(0, 2))
         add(3, slice(2, 4))
         store_y(1)
-        pack(0, CH, nc.scalar.copy)
+        pack(0, CH, nc.vector.tensor_copy)
         pack(CH, CH, nc.scalar.copy)
         store_words(0)
         pack(2 * CH, CH, nc.scalar.copy)

from contextlib import ExitStack

import concourse.mybir as mybir

K, N, T, J = 512, 512, 2048, 512
PICKS = 2
FLOPS = 2 * K * N * J * PICKS

F32 = mybir.dt.float32
BF16 = mybir.dt.bfloat16
I32 = mybir.dt.int32
U32 = mybir.dt.uint32
U16 = mybir.dt.uint16
U8 = mybir.dt.uint8
FP8X4 = mybir.dt.float8_e4m3fn_x4
ALU = mybir.AluOpType
ACT = mybir.ActivationFunctionType

P = 128
PACK = 4
GROUP = 16
HEADS = P // GROUP
HALF = 256
CH = 128
LINE = 4


def tile_list_span_resP_kernel(tc, xT, wgt, w_words, w_scales, res, offs, out_0, out_1, out_2):
    nc = tc.nc
    halves = J // HALF
    chunks = J // CH
    with ExitStack() as ctx:
        keep = ctx.enter_context(tc.tile_pool(name="keep", bufs=1))
        psum = ctx.enter_context(tc.psum_pool(name="psum", bufs=1))

        offsets = keep.tile([P, PICKS * J // GROUP], U16, name="offsets")
        nc.sync.dma_start(offsets[:], offs)

        scales_raw = keep.tile([P, N], U8, name="scales_raw", align_bytes=64)
        nc.vector.memset(scales_raw[:].bitcast(I32), 0)
        for q in range(4):
            nc.scalar.dma_start(out=scales_raw[32 * q : 32 * q + 4, :].bitcast(I32), in_=w_scales[0, 4 * q : 4 * q + 4, :].bitcast(I32))

        x_rows = xT.rearrange("(p i) t -> p i t", i=PACK)
        x_plane = [keep.tile([P, T], F32, name=f"x_plane{i}", tag=f"x_plane{i}", align_bytes=64) for i in range(PACK)]
        weight = [keep.tile([P, J], F32, name=f"weight{c}") for c in range(PICKS)]
        nc.sync.dma_start(out=weight[0][:], in_=wgt[:, 0:J])
        nc.sync.dma_start(out=x_plane[0][:], in_=x_rows[:, 0, :])
        nc.sync.dma_start(out=weight[1][:], in_=wgt[:, J : 2 * J])
        for i in range(1, PACK):
            nc.sync.dma_start(out=x_plane[i][:], in_=x_rows[:, i, :])
        words_raw = keep.tile([P, N], I32, name="words_raw", align_bytes=64)
        nc.sync.dma_start(out=words_raw[:], in_=w_words[0].rearrange("p n t -> p (n t)").bitcast(I32))
        res_rows = res.rearrange("(p i) j -> p i j", i=PACK)
        res_half = [keep.tile([P, PACK, HALF], F32, name=f"res_half{h}") for h in range(halves)]
        for h in range(halves):
            nc.sync.dma_start(out=res_half[h][:], in_=res_rows[:, :, h * HALF : (h + 1) * HALF])

        weight_neg = keep.tile([P, J], F32, name="weight_neg")
        nc.scalar.activation(out=weight_neg[:], in_=weight[1][:], func=ACT.Copy, scale=-1.0)
        signed = [weight[0], weight_neg]


        early = [keep.tile([P, 2, J], F32, name=f"early{c}") for c in range(PICKS)]
        late = keep.tile([P, 2, PICKS, J], F32, name="late")
        xb = [keep.tile([P, PICKS, CH, PACK], BF16, name=f"xb{s}", align_bytes=64) for s in range(chunks)]

        def gather(dst, i, c, j0, width):
            first = c * J + j0
            cols = offsets[:, first // GROUP : (first + width) // GROUP]
            nc.vector.tensor_tensor(dst, x_plane[i][:].indirect(cols), signed[c][:, j0 : j0 + width], ALU.mult)

        for i in range(2):
            for c in range(PICKS):
                gather(early[c][:, i, :], i, c, 0, J)
        w_scale = keep.tile([P, PACK, P], U8, name="w_scale", tag="x_plane0", align_bytes=64)
        nc.vector.tensor_copy(
            out=w_scale[:].rearrange("p t (q e) -> p q t e", e=16),
            in_=scales_raw[:].rearrange("p (q e t) -> p q t e", e=16, t=PACK),
        )
        for c in range(PICKS):
            for s in range(chunks):
                nc.scalar.copy(
                    out=xb[s][:, c, :, 0:2].rearrange("p (q e) t -> p q t e", e=LINE),
                    in_=early[c][:, :, s * CH : (s + 1) * CH].rearrange("p t (q e) -> p q t e", e=LINE),
                )
        for c in range(PICKS):
            gather(late[:, 0, c, :], 2, c, 0, J)
        for j0, width in ((0, CH), (CH, CH), (HALF, HALF)):
            for c in range(PICKS):
                gather(late[:, 1, c, j0 : j0 + width], 3, c, j0, width)

        w_code = keep.tile([P, PACK, P], I32, name="w_code", align_bytes=64)
        nc.vector.tensor_copy(
            out=w_code[:].rearrange("p t (q e) -> p q t e", e=LINE),
            in_=words_raw[:].rearrange("p (q e t) -> p q t e", e=LINE, t=PACK),
        )

        out_rows = out_0.rearrange("(p i) j -> p i j", i=PACK)
        out_words = out_1[0].rearrange("p j t -> p (j t)").bitcast(I32)
        y_scale = keep.tile([P, J], U8, name="y_scale", align_bytes=64)
        x_code = [keep.tile([P, PICKS * CH], U32, name=f"x_code{s}", align_bytes=64) for s in range(chunks)]
        x_scale = [keep.tile([P, PICKS * CH], U8, name=f"x_scale{s}", align_bytes=64) for s in range(chunks)]
        span = [keep.tile([P, PACK, CH], F32, name=f"span{s}") for s in range(chunks)]
        y = [keep.tile([P, PACK, HALF], F32, name=f"y{h}") for h in range(halves)]
        y_code = [keep.tile([P, HALF], U32, name=f"y_code{h}", align_bytes=64) for h in range(halves)]

        def front(s):
            nc.scalar.copy(
                out=xb[s][:, :, :, 2:4].rearrange("p c (q e) t -> p c q t e", e=LINE),
                in_=late[:, :, :, s * CH : (s + 1) * CH].rearrange("p t c (q e) -> p c q t e", e=LINE),
            )
            nc.vector.quantize_mx(out=x_code[s][:].bitcast(FP8X4), scales=x_scale[s][:], in_=xb[s][:].rearrange("p c j t -> p (c j t)"))

        def project(s, u):
            acc = psum.tile([P, 2, CH], F32, name=f"acc{s}_{u}", tag=f"bank{2 * s + u}")
            for t in range(2):
                for c in range(PICKS):
                    nc.tensor.matmul_mx(
                        out=acc[:, t, :],
                        lhsT=w_code[:, 2 * u + t, :].bitcast(FP8X4),
                        lhsT_scale=w_scale[:, 2 * u + t, :],
                        rhs=x_code[s][:, c * CH : (c + 1) * CH].bitcast(FP8X4),
                        rhs_scale=x_scale[s][:, c * CH : (c + 1) * CH],
                        start=(c == 0),
                        stop=(c == PICKS - 1),
                    )
            nc.scalar.activation(out=span[s][:, 2 * u : 2 * u + 2, :], in_=acc[:], func=ACT.Abs)

        def add(s, ts):
            h, j0 = divmod(s * CH, HALF)
            nc.vector.tensor_tensor(y[h][:, ts, j0 : j0 + CH], span[s][:, ts, :], res_half[h][:, ts, j0 : j0 + CH], ALU.add)

        def pack(j, width, copy):
            h, j0 = divmod(j, HALF)
            yb = keep.tile([P, width * PACK], BF16, name=f"yb{j}", align_bytes=64)
            copy(
                out=yb[:].rearrange("p (q e t) -> p q t e", e=LINE, t=PACK),
                in_=y[h][:, :, j0 : j0 + width].rearrange("p t (q e) -> p q t e", e=LINE),
            )
            nc.vector.quantize_mx(out=y_code[h][:, j0 : j0 + width].bitcast(FP8X4), scales=y_scale[:, j : j + width], in_=yb[:])

        def store_y(h):
            nc.sync.dma_start(out=out_rows[:, :, h * HALF : (h + 1) * HALF], in_=y[h][:])

        def store_words(h):
            nc.sync.dma_start(out=out_words[:, h * HALF : (h + 1) * HALF], in_=y_code[h][:].bitcast(I32))

        for s in range(chunks):
            front(s)
        for s in range(chunks):
            for u in range(2):
                project(s, u)
        whole = slice(0, PACK)
        add(0, whole)
        add(1, whole)
        store_y(0)
        add(2, whole)
        add(3, slice(0, 2))
        add(3, slice(2, 4))
        store_y(1)
        pack(0, CH, nc.vector.tensor_copy)
        pack(CH, CH, nc.scalar.copy)
        store_words(0)
        pack(2 * CH, CH, nc.scalar.copy)
        pack(3 * CH, CH, nc.vector.tensor_copy)
        store_words(1)

        for q in range(4):
            eng = nc.sync if q == 0 else nc.scalar
            eng.dma_start(out=out_2[0, 4 * q : 4 * q + 4, :].bitcast(I32), in_=y_scale[32 * q : 32 * q + 4, :].bitcast(I32))
